import numpy as np
import ml_dtypes

BF16 = ml_dtypes.bfloat16


def bf(x):
    return np.asarray(x, np.float32).astype(BF16)


def f32(x):
    return np.asarray(x, np.float32)


def f64(x):
    return np.asarray(x).astype(np.float64)


def striped(idx):
    return np.concatenate([l.reshape(-1, 16).T for l in idx])


def rows(idx, k):
    return np.tile(np.repeat(idx, 16, axis=0), (k // (16 * 8), 1))


def look(tab, idx):
    return np.take_along_axis(f64(tab), rows(idx, len(tab)), axis=1)


K, S, V, N, M = 512, 2048, 1536, 1536, 256


def setup_inputs():
    return {"tab": f32(np.random.standard_normal((K, S))), "y": f32(np.random.standard_normal((K, V))), "w": bf(np.random.standard_normal((K, M)) / np.sqrt(K)), "offs": striped(np.stack([np.random.permutation(S)[:N] for _ in range(8)]))}


def reference(tab, y, w, offs):
    idx = np.stack([g.T.reshape(-1) for g in np.split(offs, 8)])
    t = look(tab, idx)
    x = 1.0 / (1.0 + np.exp(-t)) * f64(y)
    y = f64(w).T @ x
    return y

@@ -1,0 +1,63 @@
+import concourse.mybir as mybir
+
+F32, BF16, U16 = mybir.dt.float32, mybir.dt.bfloat16, mybir.dt.uint16
+SIGMOID = mybir.ActivationFunctionType.Sigmoid
+MULT = mybir.AluOpType.mult
+
+P = 128
+GROUP = 16
+PIECE = 512
+
+K, S, N, M = 512, 2048, 1536, 256
+FLOPS = 2 * K * M * N
+
+
+def tile_lookup_gate_sig_none_kernel(tc, tab, y, w, offs, out):
+    nc = tc.nc
+    blocks, pieces, halves = K // P, N // PIECE, M // P
+
+    with (
+        tc.tile_pool(name="held", bufs=1) as held,
+        tc.tile_pool(name="ring", bufs=4) as ring,
+        tc.psum_pool(name="psum", bufs=1) as psum,
+    ):
+        offsets = held.tile([P, N // GROUP], U16, name="offsets")
+        windows = [held.tile([P, S], F32, name=f"window{b}") for b in range(blocks)]
+        streams = [held.tile([P, N], F32, name=f"stream{b}") for b in range(blocks)]
+        weights = held.tile([P, blocks, M], BF16, name="weights")
+        banks = [
+            [psum.tile([P, PIECE], F32, name=f"bank{c}_{h}") for h in range(halves)]
+            for c in range(pieces)
+        ]
+
+        nc.sync.dma_start(offsets[:], offs)
+        nc.sync.dma_start(windows[0][:], tab[0:P, :])
+        for b in range(blocks):
+            if b + 1 < blocks:
+                nc.sync.dma_start(windows[b + 1][:], tab[(b + 1) * P : (b + 2) * P, :])
+            nc.sync.dma_start(streams[b][:], y[b * P : (b + 1) * P, :])
+            if b == 0:
+                nc.sync.dma_start(weights[:], w.rearrange("(b p) m -> p b m", p=P))
+
+        for b in range(blocks):
+            for c in range(pieces):
+                columns = slice(c * PIECE, (c + 1) * PIECE)
+                entries = offsets[:, c * PIECE // GROUP : (c + 1) * PIECE // GROUP]
+                gate = ring.tile([P, PIECE], F32, name="gate")
+                nc.scalar.activation(gate[:], windows[b][:].indirect(entries), SIGMOID)
+                x = ring.tile([P, PIECE], BF16, name="x")
+                nc.vector.tensor_tensor(x[:], gate[:], streams[b][:, columns], MULT)
+                for h in range(halves):
+                    nc.tensor.matmul(
+                        banks[c][h][:],
+                        weights[:, b, h * P : (h + 1) * P],
+                        x[:],
+                        start=(b == 0),
+                        stop=(b == blocks - 1),
+                    )
+
+        for c in range(pieces):
+            for h in range(halves):
+                staged = held.tile([P, PIECE], F32, name=f"staged{c}_{h}")
+                nc.vector.tensor_copy(staged[:], banks[c][h][:])
+                nc.sync.dma_start(out[h * P : (h + 1) * P, c * PIECE : (c + 1) * PIECE], staged[:])

@@ -35,7 +35,11 @@ def tile_lookup_gate_sig_none_kernel(tc, tab, y, w, offs, out):
         for b in range(blocks):
             if b + 1 < blocks:
                 nc.sync.dma_start(windows[b + 1][:], tab[(b + 1) * P : (b + 2) * P, :])
-            nc.sync.dma_start(streams[b][:], y[b * P : (b + 1) * P, :])
+            width = N if b + 2 < blocks else PIECE
+            for first in range(0, N, width):
+                nc.sync.dma_start(
+                    streams[b][:, first : first + width], y[b * P : (b + 1) * P, first : first + width]
+                )
             if b == 0:
                 nc.sync.dma_start(weights[:], w.rearrange("(b p) m -> p b m", p=P))
 
@@ -59,5 +63,8 @@ def tile_lookup_gate_sig_none_kernel(tc, tab, y, w, offs, out):
         for c in range(pieces):
             for h in range(halves):
                 staged = held.tile([P, PIECE], F32, name=f"staged{c}_{h}")
-                nc.vector.tensor_copy(staged[:], banks[c][h][:])
+                if h == 0:
+                    nc.vector.tensor_copy(staged[:], banks[c][h][:])
+                else:
+                    nc.scalar.copy(staged[:], banks[c][h][:])
                 nc.sync.dma_start(out[h * P : (h + 1) * P, c * PIECE : (c + 1) * PIECE], staged[:])

@@ -15,56 +15,91 @@ FLOPS = 2 * K * M * N
 def tile_lookup_gate_sig_none_kernel(tc, tab, y, w, offs, out):
     nc = tc.nc
     blocks, pieces, halves = K // P, N // PIECE, M // P
+    last_block, last_piece = blocks - 1, pieces - 1
+    parts = [(0, PIECE), (PIECE, PIECE), (N - PIECE, PIECE // 2), (N - PIECE // 2, PIECE // 2)]
+    head, middle, tail_a, tail_b = parts
 
     with (
         tc.tile_pool(name="held", bufs=1) as held,
-        tc.tile_pool(name="ring", bufs=4) as ring,
+        tc.tile_pool(name="ring", bufs=2 * pieces) as ring,
         tc.psum_pool(name="psum", bufs=1) as psum,
     ):
         offsets = held.tile([P, N // GROUP], U16, name="offsets")
         windows = [held.tile([P, S], F32, name=f"window{b}") for b in range(blocks)]
         streams = [held.tile([P, N], F32, name=f"stream{b}") for b in range(blocks)]
         weights = held.tile([P, blocks, M], BF16, name="weights")
-        banks = [
-            [psum.tile([P, PIECE], F32, name=f"bank{c}_{h}") for h in range(halves)]
-            for c in range(pieces)
-        ]
+        banks = {
+            (first, h): psum.tile([P, width], F32, name=f"bank{first}_{h}")
+            for first, width in parts
+            for h in range(halves)
+        }
+        gates = {}
+
+        warm_in = held.tile([P, 8], F32, name="warm_in")
+        warm_out = held.tile([P, 8], F32, name="warm_out")
+        nc.vector.memset(warm_in[:], 0.0)
+        nc.scalar.activation(warm_out[:], warm_in[:], SIGMOID)
 
         nc.sync.dma_start(offsets[:], offs)
-        nc.sync.dma_start(windows[0][:], tab[0:P, :])
         for b in range(blocks):
-            if b + 1 < blocks:
-                nc.sync.dma_start(windows[b + 1][:], tab[(b + 1) * P : (b + 2) * P, :])
-            width = N if b + 2 < blocks else PIECE
-            for first in range(0, N, width):
-                nc.sync.dma_start(
-                    streams[b][:, first : first + width], y[b * P : (b + 1) * P, first : first + width]
-                )
-            if b == 0:
+            if b == last_block:
                 nc.sync.dma_start(weights[:], w.rearrange("(b p) m -> p b m", p=P))
+                nc.sync.dma_start(streams[0][:], y[0:P, :])
+            nc.sync.dma_start(windows[b][:], tab[b * P : (b + 1) * P, :])
+        for c in range(pieces):
+            for b in range(1, blocks):
+                columns = slice(c * PIECE, (c + 1) * PIECE)
+                nc.sync.dma_start(streams[b][:, columns], y[b * P : (b + 1) * P, columns])
+
+        def look_up(b, c):
+            entries = offsets[:, c * PIECE // GROUP : (c + 1) * PIECE // GROUP]
+            nc.scalar.activation(gates[b, c][:], windows[b][:].indirect(entries), SIGMOID)
+
+        def project(b, part):
+            first, width = part
+            c, inside = divmod(first, PIECE)
+            x = ring.tile([P, width], BF16, name="x")
+            nc.vector.tensor_tensor(
+                x[:], gates[b, c][:, inside : inside + width], streams[b][:, first : first + width], MULT
+            )
+            for h in range(halves):
+                nc.tensor.matmul(
+                    banks[first, h][:],
+                    weights[:, b, h * P : (h + 1) * P],
+                    x[:],
+                    start=(b == 0),
+                    stop=(b == last_block),
+                )
+
+        def store(part, h, copy, staged):
+            first, width = part
+            copy(staged[:, :width], banks[first, h][:])
+            nc.sync.dma_start(out[h * P : (h + 1) * P, first : first + width], staged[:, :width])
 
         for b in range(blocks):
-            for c in range(pieces):
-                columns = slice(c * PIECE, (c + 1) * PIECE)
-                entries = offsets[:, c * PIECE // GROUP : (c + 1) * PIECE // GROUP]
-                gate = ring.tile([P, PIECE], F32, name="gate")
-                nc.scalar.activation(gate[:], windows[b][:].indirect(entries), SIGMOID)
-                x = ring.tile([P, PIECE], BF16, name="x")
-                nc.vector.tensor_tensor(x[:], gate[:], streams[b][:, columns], MULT)
-                for h in range(halves):
-                    nc.tensor.matmul(
-                        banks[c][h][:],
-                        weights[:, b, h * P : (h + 1) * P],
-                        x[:],
-                        start=(b == 0),
-                        stop=(b == blocks - 1),
-                    )
+            for c in range(pieces if b < last_block - 1 else last_piece):
+                gates[b, c] = held.tile([P, PIECE], F32, name=f"gate{b}_{c}")
+                look_up(b, c)
 
-        for c in range(pieces):
-            for h in range(halves):
-                staged = held.tile([P, PIECE], F32, name=f"staged{c}_{h}")
-                if h == 0:
-                    nc.vector.tensor_copy(staged[:], banks[c][h][:])
-                else:
-                    nc.scalar.copy(staged[:], banks[c][h][:])
-                nc.sync.dma_start(out[h * P : (h + 1) * P, c * PIECE : (c + 1) * PIECE], staged[:])
+        for part in parts:
+            project(0, part)
+        for part in (head, middle):
+            for b in range(1, blocks):
+                project(b, part)
+
+        for b in (last_block - 1, last_block):
+            gates[b, last_piece] = gates[b - 1, 0]
+            look_up(b, last_piece)
+
+        for h in range(halves):
+            store(head, h, nc.vector.tensor_copy, gates[last_block - 1 + h, 1])
+        for part in (tail_a, tail_b):
+            for b in range(1, blocks):
+                project(b, part)
+
+        for h in range(halves):
+            store(middle, h, nc.scalar.copy, gates[0, h])
+        store(tail_a, 0, nc.scalar.copy, gates[0, last_piece])
+        store(tail_a, 1, nc.scalar.copy, gates[1, 1])
+        store(tail_b, 0, nc.vector.tensor_copy, gates[last_block, 0])
+        store(tail_b, 1, nc.scalar.copy, gates[1, last_piece])

import concourse.mybir as mybir

F32, BF16, U16 = mybir.dt.float32, mybir.dt.bfloat16, mybir.dt.uint16
SIGMOID = mybir.ActivationFunctionType.Sigmoid
MULT = mybir.AluOpType.mult

P = 128
GROUP = 16
PIECE = 512

K, S, N, M = 512, 2048, 1536, 256
FLOPS = 2 * K * M * N


def tile_lookup_gate_sig_none_kernel(tc, tab, y, w, offs, out):
    nc = tc.nc
    blocks, pieces, halves = K // P, N // PIECE, M // P
    last_block, last_piece = blocks - 1, pieces - 1
    parts = [(0, PIECE), (PIECE, PIECE), (N - PIECE, PIECE // 2), (N - PIECE // 2, PIECE // 2)]
    head, middle, tail_a, tail_b = parts

    with (
        tc.tile_pool(name="held", bufs=1) as held,
        tc.tile_pool(name="ring", bufs=2 * pieces) as ring,
        tc.psum_pool(name="psum", bufs=1) as psum,
    ):
        offsets = held.tile([P, N // GROUP], U16, name="offsets")
        windows = [held.tile([P, S], F32, name=f"window{b}") for b in range(blocks)]
        streams = [held.tile([P, N], F32, name=f"stream{b}") for b in range(blocks)]
        weights = held.tile([P, blocks, M], BF16, name="weights")
        banks = {
            (first, h): psum.tile([P, width], F32, name=f"bank{first}_{h}")
            for first, width in parts
            for h in range(halves)
        }
        gates = {}

        warm_in = held.tile([P, 8], F32, name="warm_in")
        warm_out = held.tile([P, 8], F32, name="warm_out")
        nc.vector.memset(warm_in[:], 0.0)
        nc.scalar.activation(warm_out[:], warm_in[:], SIGMOID)

        nc.sync.dma_start(offsets[:], offs)
        for b in range(blocks):
            if b == last_block:
                nc.sync.dma_start(weights[:], w.rearrange("(b p) m -> p b m", p=P))
                nc.sync.dma_start(streams[0][:], y[0:P, :])
            nc.sync.dma_start(windows[b][:], tab[b * P : (b + 1) * P, :])
        for c in range(pieces):
            for b in range(1, blocks):
                columns = slice(c * PIECE, (c + 1) * PIECE)
                nc.sync.dma_start(streams[b][:, columns], y[b * P : (b + 1) * P, columns])

        def look_up(b, c):
            entries = offsets[:, c * PIECE // GROUP : (c + 1) * PIECE // GROUP]
            nc.scalar.activation(gates[b, c][:], windows[b][:].indirect(entries), SIGMOID)

        def project(b, part):
            first, width = part
            c, inside = divmod(first, PIECE)
            x = ring.tile([P, width], BF16, name="x")
            nc.vector.tensor_tensor(
                x[:], gates[b, c][:, inside : inside + width], streams[b][:, first : first + width], MULT
            )
            for h in range(halves):
                nc.tensor.matmul(
                    banks[first, h][:],
                    weights[:, b, h * P : (h + 1) * P],
                    x[:],
                    start=(b == 0),
                    stop=(b == last_block),
                )

        def store(part, h, copy, staged):
            first, width = part
            copy(staged[:, :width], banks[first, h][:])
            nc.sync.dma_start(out[h * P : (h + 1) * P, first : first + width], staged[:, :width])

        for b in range(blocks):
            for c in range(pieces if b < last_block - 1 else last_piece):
                gates[b, c] = held.tile([P, PIECE], F32, name=f"gate{b}_{c}")
                look_up(b, c)

        for part in parts:
            project(0, part)
        for part in (head, middle):
            for b in range(1, blocks):
                project(b, part)

        for b in (last_block - 1, last_block):
            gates[b, last_piece] = gates[b - 1, 0]
            look_up(b, last_piece)

        for h in range(halves):
            store(head, h, nc.vector.tensor_copy, gates[last_block - 1 + h, 1])
        for part in (tail_a, tail_b):
            for b in range(1, blocks):
                project(b, part)

        for h in range(halves):
            store(middle, h, nc.scalar.copy, gates[0, h])
        store(tail_a, 0, nc.scalar.copy, gates[0, last_piece])
        store(tail_a, 1, nc.scalar.copy, gates[1, 1])
        store(tail_b, 0, nc.vector.tensor_copy, gates[last_block, 0])
        store(tail_b, 1, nc.scalar.copy, gates[1, last_piece])
